import numpy as np
import ml_dtypes


def mxq(x, axis, fmt="e4m3"):
    dtype, down = {"e4m3": (ml_dtypes.float8_e4m3fn, 7), "e5m2": (ml_dtypes.float8_e5m2, 14)}[fmt]
    v = np.moveaxis(np.asarray(x, np.float32).astype(ml_dtypes.bfloat16).astype(np.float64), axis, -1)
    blocks = v.reshape(v.shape[:-1] + (-1, 32))
    amax = np.abs(blocks).max(-1, keepdims=True)
    byte = np.maximum(np.where(amax > 0, np.frexp(amax)[1] - 1 + 127, 0) - down, 1)
    scale = np.exp2(byte - 127.0)
    codes = (blocks / scale).astype(np.float32).astype(dtype).astype(np.float64)
    return np.moveaxis((codes * scale).reshape(v.shape), -1, axis)


WIDE = False


def mx_kscale(k):
    if not WIDE:
        return np.ones(k)
    levels = np.array([10, -10, 5, -5, 0])
    if k % 512:
        return np.exp2(np.random.permutation(np.resize(levels, k // 32))).repeat(32)
    a = np.empty((k // 512, 16))
    for p in range(k // 512):
        a[p, :8] = np.random.permutation(np.resize(levels, 8))
        for g in range(8):
            far = levels[np.abs(levels - a[p, g]) >= 10]
            a[p, g + 8] = far[np.random.randint(len(far))]
    return np.exp2(a.ravel()).repeat(32)


def f64(x):
    return np.asarray(x).astype(np.float64)


def striped8(idx):
    return np.asarray(idx).reshape(8, -1, 16).transpose(0, 2, 1).reshape(128, -1).astype(np.uint16)


def unstriped8(offs):
    return offs.reshape(8, 16, -1).transpose(0, 2, 1).reshape(8, -1).astype(np.int64)


def pick8(x, idx, run):
    r = np.arange(len(x))
    return x[r[:, None], idx[r % (8 * run) // run]]


E2M1 = np.array([0.0, 0.5, 1.0, 1.5, 2.0, 3.0, 4.0, 6.0, -0.0, -0.5, -1.0, -1.5, -2.0, -3.0, -4.0, -6.0])


def pack_weight(w, fmt):
    k, n = w.shape
    w = f64(np.asarray(w, np.float32).astype(ml_dtypes.bfloat16)).reshape(k // 32, 32, n)
    amax = np.abs(w).max(1)
    if fmt == "e4m3":
        byte = np.frexp(amax)[1] - 1 + 127 - 7
    else:
        mant, ex = np.frexp(amax / 6.0)
        byte = np.where(mant > 0.5, ex, ex - 1) + 127
    byte = np.clip(np.where(amax > 0, byte, 1), 1, 254)
    scaled = (w * np.exp2(127.0 - byte)[:, None, :]).reshape(k, n).astype(np.float32)
    by_word = np.ascontiguousarray(scaled.reshape(k // 512, 128, 4, n).transpose(0, 1, 3, 2))
    if fmt == "e4m3":
        words = by_word.astype(ml_dtypes.float8_e4m3fn).view(np.uint8)
    else:
        c = by_word.astype(ml_dtypes.float4_e2m1fn).view(np.uint8) & 0xF
        words = (c[..., 0::2] | (c[..., 1::2] << 4)).reshape(k // 512, 128, 2 * n)
    return np.ascontiguousarray(words), np.ascontiguousarray(byte.astype(np.uint8).reshape(k // 512, 16, n))


def unpack_weight(words, scales, fmt):
    g, _, n = scales.shape
    words = np.ascontiguousarray(words).reshape(g, 128, n, -1)
    if fmt == "e4m3":
        vals = words.view(ml_dtypes.float8_e4m3fn).astype(np.float64)
    else:
        nib = np.empty((g, 128, n, 4), np.uint8)
        nib[..., 0::2] = words & 0xF
        nib[..., 1::2] = words >> 4
        vals = E2M1[nib]
    vals = vals * np.repeat(np.exp2(scales.astype(np.float64) - 127.0), 8, axis=1)[..., None]
    return vals.transpose(0, 1, 3, 2).reshape(g * 512, n)


D, T, I, Q = 512, 1024, 512, 128


def setup_inputs():
    n = np.random.standard_normal
    idx = np.stack([np.random.permutation(T)[:I] for _ in range(8)])
    idx2 = np.stack([np.random.permutation(T)[:I] for _ in range(8)])
    idx3 = np.stack([np.random.permutation(T)[:I] for _ in range(8)])
    fd = mx_kscale(D)
    keysp = pack_weight(n((D, T)) / fd[:, None], "e2m1")
    return {
        "query": (n((D, Q)) * 0.9 / np.sqrt(D) * fd[:, None]).astype(np.float32),
        "query2": (n((D, Q)) * 0.9 / np.sqrt(D) * fd[:, None]).astype(np.float32),
        "keys_words": keysp[0],
        "keys_scales": keysp[1],
        "lam": (np.random.uniform(0.5, 1.3, (Q, 1))).astype(np.float32),
        "old": (1.0 * n((Q, T))).astype(np.float32),
        "offs": striped8(idx),
        "offs2": striped8(idx2),
        "offs3": striped8(idx3),
    }


def reference(query, query2, keys_words, keys_scales, lam, old, offs, offs2, offs3):
    idx = unstriped8(offs)
    idx2 = unstriped8(offs2)
    idx3 = unstriped8(offs3)
    keysu = unpack_weight(keys_words, keys_scales, "e2m1")
    queryq = mxq(f64(query), 0, "e4m3")
    a = queryq.T @ keysu
    query2q = mxq(f64(query2), 0, "e4m3")
    b = query2q.T @ keysu
    w = (np.maximum(pick8(a, idx, 16), pick8(b, idx2, 16)) - np.maximum(pick8(a, idx2, 16), pick8(b, idx, 16))) * f64(lam)
    f1 = np.zeros((Q, T))
    f1[np.arange(Q)[:, None], idx[np.arange(Q) % 128 // 16]] = w
    f2 = f1 + f64(old)
    y = pick8(f2, idx3, 16) * w
    return y

@@ -1,0 +1,124 @@
+from contextlib import ExitStack
+
+import concourse.mybir as mybir
+
+D, T, I, Q = 512, 1024, 512, 128
+FLOPS = 2 * 2 * D * Q * T
+
+F32 = mybir.dt.float32
+BF16 = mybir.dt.bfloat16
+I32 = mybir.dt.int32
+U32 = mybir.dt.uint32
+U16 = mybir.dt.uint16
+U8 = mybir.dt.uint8
+FP8X4 = mybir.dt.float8_e4m3fn_x4
+FP4X4 = mybir.dt.float4_e2m1fn_x4
+ALU = mybir.AluOpType
+COPY = mybir.ActivationFunctionType.Copy
+
+P = 128
+PACK = 4
+N_TILE = 256
+HALF = I // 2
+LIST_COLS = HALF // 16
+
+
+def tile_attend_exchanged_lean_throughtimes_heads_kernel(
+    tc, query, query2, keys_words, keys_scales, lam, old, offs, offs2, offs3, out
+):
+    nc = tc.nc
+    with ExitStack() as ctx:
+        sb = ctx.enter_context(tc.tile_pool(name="sb", bufs=1))
+        psum = ctx.enter_context(tc.psum_pool(name="psum", bufs=1))
+
+        list1 = sb.tile([P, I // 16], U16, name="list1")
+        list2 = sb.tile([P, I // 16], U16, name="list2")
+        list3 = sb.tile([P, I // 16], U16, name="list3")
+        raw = [sb.tile([P, PACK, Q], F32, name=f"raw{j}") for j in range(2)]
+        words = sb.tile([P, 2 * T], U8, name="words", tag="words_then_a", align_bytes=64)
+        key_scales = sb.tile([P, T], U8, name="key_scales", tag="scales_then_lam", align_bytes=64)
+        lam_col = sb.tile([P, 1], F32, name="lam_col")
+        old_sb = sb.tile([P, T], F32, name="old_sb")
+        f1 = sb.tile([P, T], F32, name="f1")
+
+        nc.vector.memset(key_scales[:].bitcast(U32), 0)
+        nc.sync.dma_start(out=raw[0][:], in_=query.rearrange("(p j) w -> p j w", j=PACK))
+        nc.sync.dma_start(out=words[:].bitcast(I32), in_=keys_words[0].bitcast(I32))
+        for quad in range(4):
+            nc.scalar.dma_start(
+                out=key_scales[32 * quad : 32 * quad + 4, :].bitcast(I32),
+                in_=keys_scales[0, 4 * quad : 4 * quad + 4, :].bitcast(I32),
+            )
+        nc.sync.dma_start(out=raw[1][:], in_=query2.rearrange("(p j) w -> p j w", j=PACK))
+        nc.sync.dma_start(out=list1[:], in_=offs)
+        nc.sync.dma_start(out=list2[:], in_=offs2)
+        nc.sync.dma_start(out=lam_col[:], in_=lam)
+        nc.sync.dma_start(out=old_sb[:], in_=old)
+        nc.sync.dma_start(out=list3[:], in_=offs3)
+        nc.vector.memset(f1[:], 0.0)
+
+
+        scores = []
+        for j in range(2):
+            grouped = sb.tile([P, Q, PACK], BF16, name=f"grouped{j}", align_bytes=64)
+            nc.vector.tensor_copy(out=grouped[:], in_=raw[j][:].rearrange("p j w -> p w j"))
+            codes = sb.tile([P, Q], U32, name=f"codes{j}", align_bytes=64)
+            q_scales = sb.tile([P, Q], U8, name=f"q_scales{j}", align_bytes=64)
+            nc.vector.quantize_mx(
+                out=codes[:].bitcast(FP8X4), scales=q_scales[:], in_=grouped[:].rearrange("p w j -> p (w j)")
+            )
+            score = sb.tile([P, T], F32, name=f"score{j}")
+            for n0 in range(0, T, N_TILE):
+                acc = psum.tile([P, N_TILE], F32, name=f"acc{j}_{n0}")
+                nc.tensor.matmul_mx(
+                    out=acc[:],
+                    lhsT=codes[:].bitcast(FP8X4),
+                    lhsT_scale=q_scales[:],
+                    rhs=words[:, 2 * n0 : 2 * (n0 + N_TILE)].bitcast(FP4X4),
+                    rhs_scale=key_scales[:, n0 : n0 + N_TILE],
+                    start=True,
+                    stop=True,
+                )
+                nc.scalar.activation(out=score[:, n0 : n0 + N_TILE], in_=acc[:], func=COPY)
+            scores.append(score)
+        a, b = scores
+
+        cols = [slice(h * LIST_COLS, (h + 1) * LIST_COLS) for h in range(2)]
+        slots = [slice(h * HALF, (h + 1) * HALF) for h in range(2)]
+        from_a = [
+            sb.tile([P, 2, HALF], F32, name="from_a0"),
+            sb.tile([P, 2, HALF], F32, name="from_a1", tag="words_then_a", align_bytes=64),
+        ]
+        from_b = [sb.tile([P, 2, HALF], F32, name=f"from_b{h}") for h in range(2)]
+        nc.vector.tensor_copy(out=from_a[0][:, 0, :], in_=a[:].indirect(list1[:, cols[0]]))
+        nc.vector.tensor_copy(out=from_a[0][:, 1, :], in_=a[:].indirect(list2[:, cols[0]]))
+        nc.vector.tensor_copy(out=from_b[0][:, 0, :], in_=b[:].indirect(list2[:, cols[0]]))
+        nc.vector.tensor_copy(out=from_b[0][:, 1, :], in_=b[:].indirect(list1[:, cols[0]]))
+        nc.scalar.activation(out=from_a[1][:, 0, :], in_=a[:].indirect(list1[:, cols[1]]), func=COPY)
+        nc.scalar.activation(out=from_a[1][:, 1, :], in_=a[:].indirect(list2[:, cols[1]]), func=COPY)
+        nc.scalar.activation(out=from_b[1][:, 0, :], in_=b[:].indirect(list2[:, cols[1]]), func=COPY)
+        nc.scalar.activation(out=from_b[1][:, 1, :], in_=b[:].indirect(list1[:, cols[1]]), func=COPY)
+        lam_wide = sb.tile([P, HALF], F32, name="lam_wide", tag="scales_then_lam", align_bytes=64)
+        nc.scalar.activation(out=lam_wide[:], in_=lam_col[:].to_broadcast([P, HALF]), func=COPY)
+        diff = sb.tile([P, I], F32, name="diff")
+        for h in range(2):
+            larger = sb.tile([P, 2, HALF], F32, name=f"larger{h}", tag="larger")
+            nc.vector.tensor_tensor(out=larger[:], in0=from_a[h][:], in1=from_b[h][:], op=ALU.max)
+            nc.vector.tensor_tensor(out=diff[:, slots[h]], in0=larger[:, 0, :], in1=larger[:, 1, :], op=ALU.subtract)
+            nc.vector.tensor_tensor(
+                out=f1[:].indirect(list1[:, cols[h]]), in0=diff[:, slots[h]], in1=lam_wide[:], op=ALU.mult
+            )
+        w = sb.tile([P, I], F32, name="w")
+        nc.scalar.activation(out=w[:], in_=diff[:], func=COPY, scale=lam_col[:])
+
+        f2 = sb.tile([P, T], F32, name="f2")
+        nc.vector.tensor_tensor(out=f2[:], in0=f1[:], in1=old_sb[:], op=ALU.add)
+
+        res0 = sb.tile([P, HALF], F32, name="res0")
+        res1 = sb.tile([P, HALF], F32, name="res1")
+        picked = sb.tile([P, HALF], F32, name="picked")
+        nc.vector.tensor_tensor(out=res0[:], in0=f2[:].indirect(list3[:, 0:LIST_COLS]), in1=w[:, 0:HALF], op=ALU.mult)
+        nc.scalar.activation(out=picked[:], in_=f2[:].indirect(list3[:, LIST_COLS : 2 * LIST_COLS]), func=COPY)
+        nc.sync.dma_start(out=out[:, 0:HALF], in_=res0[:])
+        nc.vector.tensor_tensor(out=res1[:], in0=picked[:], in1=w[:, HALF:I], op=ALU.mult)
+        nc.sync.dma_start(out=out[:, HALF:I], in_=res1[:])

@@ -36,16 +36,16 @@ def tile_attend_exchanged_lean_throughtimes_heads_kernel(
         list3 = sb.tile([P, I // 16], U16, name="list3")
         raw = [sb.tile([P, PACK, Q], F32, name=f"raw{j}") for j in range(2)]
         words = sb.tile([P, 2 * T], U8, name="words", tag="words_then_a", align_bytes=64)
-        key_scales = sb.tile([P, T], U8, name="key_scales", tag="scales_then_lam", align_bytes=64)
+        key_scales = sb.tile([P, T], U8, name="key_scales", align_bytes=64)
         lam_col = sb.tile([P, 1], F32, name="lam_col")
         old_sb = sb.tile([P, T], F32, name="old_sb")
         f1 = sb.tile([P, T], F32, name="f1")
 
-        nc.vector.memset(key_scales[:].bitcast(U32), 0)
         nc.sync.dma_start(out=raw[0][:], in_=query.rearrange("(p j) w -> p j w", j=PACK))
         nc.sync.dma_start(out=words[:].bitcast(I32), in_=keys_words[0].bitcast(I32))
         for quad in range(4):
-            nc.scalar.dma_start(
+            queue = nc.scalar if quad < 2 else nc.sync
+            queue.dma_start(
                 out=key_scales[32 * quad : 32 * quad + 4, :].bitcast(I32),
                 in_=keys_scales[0, 4 * quad : 4 * quad + 4, :].bitcast(I32),
             )
@@ -61,12 +61,17 @@ def tile_attend_exchanged_lean_throughtimes_heads_kernel(
         scores = []
         for j in range(2):
             grouped = sb.tile([P, Q, PACK], BF16, name=f"grouped{j}", align_bytes=64)
-            nc.vector.tensor_copy(out=grouped[:], in_=raw[j][:].rearrange("p j w -> p w j"))
             codes = sb.tile([P, Q], U32, name=f"codes{j}", align_bytes=64)
             q_scales = sb.tile([P, Q], U8, name=f"q_scales{j}", align_bytes=64)
-            nc.vector.quantize_mx(
-                out=codes[:].bitcast(FP8X4), scales=q_scales[:], in_=grouped[:].rearrange("p w j -> p (w j)")
-            )
+            pieces = [slice(0, Q // 2), slice(Q // 2, Q)]
+            for rows in pieces:
+                nc.vector.tensor_copy(out=grouped[:, rows, :], in_=raw[j][:, :, rows].rearrange("p j w -> p w j"))
+            for rows in pieces:
+                nc.vector.quantize_mx(
+                    out=codes[:, rows].bitcast(FP8X4),
+                    scales=q_scales[:, rows],
+                    in_=grouped[:, rows, :].rearrange("p w j -> p (w j)"),
+                )
             score = sb.tile([P, T], F32, name=f"score{j}")
             for n0 in range(0, T, N_TILE):
                 acc = psum.tile([P, N_TILE], F32, name=f"acc{j}_{n0}")
@@ -79,35 +84,54 @@ def tile_attend_exchanged_lean_throughtimes_heads_kernel(
                     start=True,
                     stop=True,
                 )
-                nc.scalar.activation(out=score[:, n0 : n0 + N_TILE], in_=acc[:], func=COPY)
+                if j == 0 and n0 == T - N_TILE:
+                    nc.vector.tensor_copy(out=score[:, n0 : n0 + N_TILE], in_=acc[:])
+                else:
+                    nc.scalar.activation(out=score[:, n0 : n0 + N_TILE], in_=acc[:], func=COPY)
             scores.append(score)
         a, b = scores
 
         cols = [slice(h * LIST_COLS, (h + 1) * LIST_COLS) for h in range(2)]
         slots = [slice(h * HALF, (h + 1) * HALF) for h in range(2)]
+        lam_wide = sb.tile([P, HALF], F32, name="lam_wide")
+        nc.gpsimd.tensor_copy(out=lam_wide[:], in_=lam_col[:].to_broadcast([P, HALF]))
         from_a = [
             sb.tile([P, 2, HALF], F32, name="from_a0"),
             sb.tile([P, 2, HALF], F32, name="from_a1", tag="words_then_a", align_bytes=64),
         ]
         from_b = [sb.tile([P, 2, HALF], F32, name=f"from_b{h}") for h in range(2)]
-        nc.vector.tensor_copy(out=from_a[0][:, 0, :], in_=a[:].indirect(list1[:, cols[0]]))
-        nc.vector.tensor_copy(out=from_a[0][:, 1, :], in_=a[:].indirect(list2[:, cols[0]]))
-        nc.vector.tensor_copy(out=from_b[0][:, 0, :], in_=b[:].indirect(list2[:, cols[0]]))
-        nc.vector.tensor_copy(out=from_b[0][:, 1, :], in_=b[:].indirect(list1[:, cols[0]]))
-        nc.scalar.activation(out=from_a[1][:, 0, :], in_=a[:].indirect(list1[:, cols[1]]), func=COPY)
-        nc.scalar.activation(out=from_a[1][:, 1, :], in_=a[:].indirect(list2[:, cols[1]]), func=COPY)
-        nc.scalar.activation(out=from_b[1][:, 0, :], in_=b[:].indirect(list2[:, cols[1]]), func=COPY)
-        nc.scalar.activation(out=from_b[1][:, 1, :], in_=b[:].indirect(list1[:, cols[1]]), func=COPY)
-        lam_wide = sb.tile([P, HALF], F32, name="lam_wide", tag="scales_then_lam", align_bytes=64)
-        nc.scalar.activation(out=lam_wide[:], in_=lam_col[:].to_broadcast([P, HALF]), func=COPY)
+        larger = [sb.tile([P, 2, HALF], F32, name=f"larger{h}") for h in range(2)]
         diff = sb.tile([P, I], F32, name="diff")
-        for h in range(2):
-            larger = sb.tile([P, 2, HALF], F32, name=f"larger{h}", tag="larger")
-            nc.vector.tensor_tensor(out=larger[:], in0=from_a[h][:], in1=from_b[h][:], op=ALU.max)
-            nc.vector.tensor_tensor(out=diff[:, slots[h]], in0=larger[:, 0, :], in1=larger[:, 1, :], op=ALU.subtract)
+        lists = [list1, list2]
+        for s in range(2):
+            nc.vector.tensor_copy(out=from_a[0][:, s, :], in_=a[:].indirect(lists[s][:, cols[0]]))
+        for s in range(2):
+            nc.vector.tensor_copy(out=from_b[0][:, s, :], in_=b[:].indirect(lists[1 - s][:, cols[0]]))
+        for s in range(2):
+            nc.scalar.activation(out=from_a[1][:, s, :], in_=a[:].indirect(lists[s][:, cols[1]]), func=COPY)
+            nc.scalar.activation(out=from_b[1][:, s, :], in_=b[:].indirect(lists[1 - s][:, cols[1]]), func=COPY)
+
+        def take_larger(h, s):
+            nc.vector.tensor_tensor(out=larger[h][:, s, :], in0=from_a[h][:, s, :], in1=from_b[h][:, s, :], op=ALU.max)
+
+        def subtract(h):
+            nc.vector.tensor_tensor(
+                out=diff[:, slots[h]], in0=larger[h][:, 0, :], in1=larger[h][:, 1, :], op=ALU.subtract
+            )
+
+        def scatter(h):
             nc.vector.tensor_tensor(
                 out=f1[:].indirect(list1[:, cols[h]]), in0=diff[:, slots[h]], in1=lam_wide[:], op=ALU.mult
             )
+
+        take_larger(0, 0)
+        take_larger(0, 1)
+        take_larger(1, 0)
+        subtract(0)
+        take_larger(1, 1)
+        scatter(0)
+        subtract(1)
+        scatter(1)
         w = sb.tile([P, I], F32, name="w")
         nc.scalar.activation(out=w[:], in_=diff[:], func=COPY, scale=lam_col[:])
 

@@ -35,21 +35,25 @@ def tile_attend_exchanged_lean_throughtimes_heads_kernel(
         list2 = sb.tile([P, I // 16], U16, name="list2")
         list3 = sb.tile([P, I // 16], U16, name="list3")
         raw = [sb.tile([P, PACK, Q], F32, name=f"raw{j}") for j in range(2)]
-        words = sb.tile([P, 2 * T], U8, name="words", tag="words_then_a", align_bytes=64)
+        words = [
+            sb.tile([P, T], U8, name="words0", align_bytes=64),
+            sb.tile([P, T], U8, name="words1", tag="words_then_a", align_bytes=64),
+        ]
         key_scales = sb.tile([P, T], U8, name="key_scales", align_bytes=64)
         lam_col = sb.tile([P, 1], F32, name="lam_col")
         old_sb = sb.tile([P, T], F32, name="old_sb")
         f1 = sb.tile([P, T], F32, name="f1")
 
         nc.sync.dma_start(out=raw[0][:], in_=query.rearrange("(p j) w -> p j w", j=PACK))
-        nc.sync.dma_start(out=words[:].bitcast(I32), in_=keys_words[0].bitcast(I32))
         for quad in range(4):
             queue = nc.scalar if quad < 2 else nc.sync
             queue.dma_start(
                 out=key_scales[32 * quad : 32 * quad + 4, :].bitcast(I32),
                 in_=keys_scales[0, 4 * quad : 4 * quad + 4, :].bitcast(I32),
             )
+        nc.sync.dma_start(out=words[0][:].bitcast(I32), in_=keys_words[0, :, 0:T].bitcast(I32))
         nc.sync.dma_start(out=raw[1][:], in_=query2.rearrange("(p j) w -> p j w", j=PACK))
+        nc.sync.dma_start(out=words[1][:].bitcast(I32), in_=keys_words[0, :, T : 2 * T].bitcast(I32))
         nc.sync.dma_start(out=list1[:], in_=offs)
         nc.sync.dma_start(out=list2[:], in_=offs2)
         nc.sync.dma_start(out=lam_col[:], in_=lam)
@@ -59,6 +63,7 @@ def tile_attend_exchanged_lean_throughtimes_heads_kernel(
 
 
         scores = []
+        stationary = []
         for j in range(2):
             grouped = sb.tile([P, Q, PACK], BF16, name=f"grouped{j}", align_bytes=64)
             codes = sb.tile([P, Q], U32, name=f"codes{j}", align_bytes=64)
@@ -72,6 +77,9 @@ def tile_attend_exchanged_lean_throughtimes_heads_kernel(
                     scales=q_scales[:, rows],
                     in_=grouped[:, rows, :].rearrange("p w j -> p (w j)"),
                 )
+            stationary.append((codes, q_scales))
+
+        for j, (codes, q_scales) in enumerate(stationary):
             score = sb.tile([P, T], F32, name=f"score{j}")
             for n0 in range(0, T, N_TILE):
                 acc = psum.tile([P, N_TILE], F32, name=f"acc{j}_{n0}")
@@ -79,7 +87,7 @@ def tile_attend_exchanged_lean_throughtimes_heads_kernel(
                     out=acc[:],
                     lhsT=codes[:].bitcast(FP8X4),
                     lhsT_scale=q_scales[:],
-                    rhs=words[:, 2 * n0 : 2 * (n0 + N_TILE)].bitcast(FP4X4),
+                    rhs=words[2 * n0 // T][:, 2 * n0 % T : 2 * n0 % T + 2 * N_TILE].bitcast(FP4X4),
                     rhs_scale=key_scales[:, n0 : n0 + N_TILE],
                     start=True,
                     stop=True,
@@ -93,10 +101,8 @@ def tile_attend_exchanged_lean_throughtimes_heads_kernel(
 
         cols = [slice(h * LIST_COLS, (h + 1) * LIST_COLS) for h in range(2)]
         slots = [slice(h * HALF, (h + 1) * HALF) for h in range(2)]
-        lam_wide = sb.tile([P, HALF], F32, name="lam_wide")
-        nc.gpsimd.tensor_copy(out=lam_wide[:], in_=lam_col[:].to_broadcast([P, HALF]))
         from_a = [
-            sb.tile([P, 2, HALF], F32, name="from_a0"),
+            sb.tile([P, 2, HALF], F32, name="from_a0", tag="a_then_lam"),
             sb.tile([P, 2, HALF], F32, name="from_a1", tag="words_then_a", align_bytes=64),
         ]
         from_b = [sb.tile([P, 2, HALF], F32, name=f"from_b{h}") for h in range(2)]
@@ -126,6 +132,8 @@ def tile_attend_exchanged_lean_throughtimes_heads_kernel(
 
         take_larger(0, 0)
         take_larger(0, 1)
+        lam_wide = sb.tile([P, HALF], F32, name="lam_wide", tag="a_then_lam")
+        nc.scalar.activation(out=lam_wide[:], in_=lam_col[:].to_broadcast([P, HALF]), func=COPY)
         take_larger(1, 0)
         subtract(0)
         take_larger(1, 1)

@@ -69,9 +69,11 @@ def tile_attend_exchanged_lean_throughtimes_heads_kernel(
             codes = sb.tile([P, Q], U32, name=f"codes{j}", align_bytes=64)
             q_scales = sb.tile([P, Q], U8, name=f"q_scales{j}", align_bytes=64)
             pieces = [slice(0, Q // 2), slice(Q // 2, Q)]
-            for rows in pieces:
-                nc.vector.tensor_copy(out=grouped[:, rows, :], in_=raw[j][:, :, rows].rearrange("p j w -> p w j"))
-            for rows in pieces:
+            nc.vector.tensor_copy(out=grouped[:, pieces[0], :], in_=raw[j][:, :, pieces[0]].rearrange("p j w -> p w j"))
+            nc.scalar.activation(
+                out=grouped[:, pieces[1], :], in_=raw[j][:, :, pieces[1]].rearrange("p j w -> p w j"), func=COPY
+            )
+            for rows in reversed(pieces):
                 nc.vector.quantize_mx(
                     out=codes[:, rows].bitcast(FP8X4),
                     scales=q_scales[:, rows],
@@ -92,7 +94,7 @@ def tile_attend_exchanged_lean_throughtimes_heads_kernel(
                     start=True,
                     stop=True,
                 )
-                if j == 0 and n0 == T - N_TILE:
+                if j == 0 and n0 == T - 2 * N_TILE:
                     nc.vector.tensor_copy(out=score[:, n0 : n0 + N_TILE], in_=acc[:])
                 else:
                     nc.scalar.activation(out=score[:, n0 : n0 + N_TILE], in_=acc[:], func=COPY)
@@ -107,7 +109,7 @@ def tile_attend_exchanged_lean_throughtimes_heads_kernel(
         ]
         from_b = [sb.tile([P, 2, HALF], F32, name=f"from_b{h}") for h in range(2)]
         larger = [sb.tile([P, 2, HALF], F32, name=f"larger{h}") for h in range(2)]
-        diff = sb.tile([P, I], F32, name="diff")
+        diff = sb.tile([P, HALF], F32, name="diff")
         lists = [list1, list2]
         for s in range(2):
             nc.vector.tensor_copy(out=from_a[0][:, s, :], in_=a[:].indirect(lists[s][:, cols[0]]))
@@ -120,28 +122,25 @@ def tile_attend_exchanged_lean_throughtimes_heads_kernel(
         def take_larger(h, s):
             nc.vector.tensor_tensor(out=larger[h][:, s, :], in0=from_a[h][:, s, :], in1=from_b[h][:, s, :], op=ALU.max)
 
-        def subtract(h):
-            nc.vector.tensor_tensor(
-                out=diff[:, slots[h]], in0=larger[h][:, 0, :], in1=larger[h][:, 1, :], op=ALU.subtract
-            )
-
-        def scatter(h):
-            nc.vector.tensor_tensor(
-                out=f1[:].indirect(list1[:, cols[h]]), in0=diff[:, slots[h]], in1=lam_wide[:], op=ALU.mult
-            )
-
+        w = sb.tile([P, I], F32, name="w")
         take_larger(0, 0)
         take_larger(0, 1)
         lam_wide = sb.tile([P, HALF], F32, name="lam_wide", tag="a_then_lam")
         nc.scalar.activation(out=lam_wide[:], in_=lam_col[:].to_broadcast([P, HALF]), func=COPY)
         take_larger(1, 0)
-        subtract(0)
+        nc.vector.tensor_tensor(out=diff[:], in0=larger[0][:, 0, :], in1=larger[0][:, 1, :], op=ALU.subtract)
         take_larger(1, 1)
-        scatter(0)
-        subtract(1)
-        scatter(1)
-        w = sb.tile([P, I], F32, name="w")
-        nc.scalar.activation(out=w[:], in_=diff[:], func=COPY, scale=lam_col[:])
+        nc.vector.tensor_tensor(out=f1[:].indirect(list1[:, cols[0]]), in0=diff[:], in1=lam_wide[:], op=ALU.mult)
+        minus_lam = sb.tile([P, 1], F32, name="minus_lam")
+        nc.scalar.activation(out=minus_lam[:], in_=lam_wide[:, 0:1], func=COPY, scale=-1.0)
+        terms = sb.tile([P, 2, HALF], F32, name="terms")
+        nc.scalar.activation(out=terms[:, 0, :], in_=larger[1][:, 0, :], func=COPY, scale=lam_col[:])
+        nc.scalar.activation(out=terms[:, 1, :], in_=larger[1][:, 1, :], func=COPY, scale=minus_lam[:])
+        nc.scalar.activation(out=w[:, slots[0]], in_=diff[:], func=COPY, scale=lam_col[:])
+        nc.vector.tensor_tensor(out=w[:, slots[1]], in0=terms[:, 0, :], in1=terms[:, 1, :], op=ALU.add)
+        nc.vector.tensor_tensor(
+            out=f1[:].indirect(list1[:, cols[1]]), in0=terms[:, 0, :], in1=terms[:, 1, :], op=ALU.add
+        )
 
         f2 = sb.tile([P, T], F32, name="f2")
         nc.vector.tensor_tensor(out=f2[:], in0=f1[:], in1=old_sb[:], op=ALU.add)

@@ -1,6 +1,7 @@
 from contextlib import ExitStack
 
 import concourse.mybir as mybir
+from concourse.masks import make_identity
 
 D, T, I, Q = 512, 1024, 512, 128
 FLOPS = 2 * 2 * D * Q * T
@@ -62,6 +63,8 @@ def tile_attend_exchanged_lean_throughtimes_heads_kernel(
         nc.vector.memset(f1[:], 0.0)
 
 
+        ident = sb.tile([P, P], F32, name="ident")
+        make_identity(nc, ident[:])
         scores = []
         stationary = []
         for j in range(2):
@@ -107,7 +110,10 @@ def tile_attend_exchanged_lean_throughtimes_heads_kernel(
             sb.tile([P, 2, HALF], F32, name="from_a0", tag="a_then_lam"),
             sb.tile([P, 2, HALF], F32, name="from_a1", tag="words_then_a", align_bytes=64),
         ]
-        from_b = [sb.tile([P, 2, HALF], F32, name=f"from_b{h}") for h in range(2)]
+        from_b = [
+            sb.tile([P, 2, HALF], F32, name="from_b0"),
+            sb.tile([P, 2, HALF], F32, name="from_b1", tag="b_then_old"),
+        ]
         larger = [sb.tile([P, 2, HALF], F32, name=f"larger{h}") for h in range(2)]
         diff = sb.tile([P, HALF], F32, name="diff")
         lists = [list1, list2]
@@ -137,13 +143,28 @@ def tile_attend_exchanged_lean_throughtimes_heads_kernel(
         nc.scalar.activation(out=terms[:, 0, :], in_=larger[1][:, 0, :], func=COPY, scale=lam_col[:])
         nc.scalar.activation(out=terms[:, 1, :], in_=larger[1][:, 1, :], func=COPY, scale=minus_lam[:])
         nc.scalar.activation(out=w[:, slots[0]], in_=diff[:], func=COPY, scale=lam_col[:])
+        spans = [(0, 512), (512, 640)]
+        old_turned = sb.tile([P, 640], F32, name="old_turned", tag="b_then_old")
+        old_psum = []
+        for u, (c0, c1) in enumerate(spans):
+            turned = psum.tile([P, c1 - c0], F32, name=f"turned{u}", tag=f"acc0_{256 * u}")
+            for c in range(c0, c1, P):
+                nc.tensor.transpose(turned[:, c - c0 : c - c0 + P], old_sb[:, c : c + P], ident[:])
+            nc.scalar.activation(out=old_turned[:, c0:c1], in_=turned[:], func=COPY)
+        for u, (c0, c1) in enumerate(spans):
+            back = psum.tile([P, c1 - c0], F32, name=f"back{u}", tag=f"acc0_{256 * (u + 2)}")
+            for c in range(c0, c1, P):
+                nc.tensor.transpose(back[:, c - c0 : c - c0 + P], old_turned[:, c : c + P], ident[:])
+            old_psum.append(back)
         nc.vector.tensor_tensor(out=w[:, slots[1]], in0=terms[:, 0, :], in1=terms[:, 1, :], op=ALU.add)
         nc.vector.tensor_tensor(
             out=f1[:].indirect(list1[:, cols[1]]), in0=terms[:, 0, :], in1=terms[:, 1, :], op=ALU.add
         )
 
         f2 = sb.tile([P, T], F32, name="f2")
-        nc.vector.tensor_tensor(out=f2[:], in0=f1[:], in1=old_sb[:], op=ALU.add)
+        nc.gpsimd.tensor_tensor(out=f2[:, 640:T], in0=f1[:, 640:T], in1=old_sb[:, 640:T], op=ALU.add)
+        for (c0, c1), back in zip(spans, old_psum):
+            nc.vector.tensor_tensor(out=f2[:, c0:c1], in0=f1[:, c0:c1], in1=back[:], op=ALU.add)
 
         res0 = sb.tile([P, HALF], F32, name="res0")
         res1 = sb.tile([P, HALF], F32, name="res1")

from contextlib import ExitStack

import concourse.mybir as mybir
from concourse.masks import make_identity

D, T, I, Q = 512, 1024, 512, 128
FLOPS = 2 * 2 * D * Q * T

F32 = mybir.dt.float32
BF16 = mybir.dt.bfloat16
I32 = mybir.dt.int32
U32 = mybir.dt.uint32
U16 = mybir.dt.uint16
U8 = mybir.dt.uint8
FP8X4 = mybir.dt.float8_e4m3fn_x4
FP4X4 = mybir.dt.float4_e2m1fn_x4
ALU = mybir.AluOpType
COPY = mybir.ActivationFunctionType.Copy

P = 128
PACK = 4
N_TILE = 256
HALF = I // 2
LIST_COLS = HALF // 16


def tile_attend_exchanged_lean_throughtimes_heads_kernel(
    tc, query, query2, keys_words, keys_scales, lam, old, offs, offs2, offs3, out
):
    nc = tc.nc
    with ExitStack() as ctx:
        sb = ctx.enter_context(tc.tile_pool(name="sb", bufs=1))
        psum = ctx.enter_context(tc.psum_pool(name="psum", bufs=1))

        list1 = sb.tile([P, I // 16], U16, name="list1")
        list2 = sb.tile([P, I // 16], U16, name="list2")
        list3 = sb.tile([P, I // 16], U16, name="list3")
        raw = [sb.tile([P, PACK, Q], F32, name=f"raw{j}") for j in range(2)]
        words = [
            sb.tile([P, T], U8, name="words0", align_bytes=64),
            sb.tile([P, T], U8, name="words1", tag="words_then_a", align_bytes=64),
        ]
        key_scales = sb.tile([P, T], U8, name="key_scales", align_bytes=64)
        lam_col = sb.tile([P, 1], F32, name="lam_col")
        old_sb = sb.tile([P, T], F32, name="old_sb")
        f1 = sb.tile([P, T], F32, name="f1")

        nc.sync.dma_start(out=raw[0][:], in_=query.rearrange("(p j) w -> p j w", j=PACK))
        for quad in range(4):
            queue = nc.scalar if quad < 2 else nc.sync
            queue.dma_start(
                out=key_scales[32 * quad : 32 * quad + 4, :].bitcast(I32),
                in_=keys_scales[0, 4 * quad : 4 * quad + 4, :].bitcast(I32),
            )
        nc.sync.dma_start(out=words[0][:].bitcast(I32), in_=keys_words[0, :, 0:T].bitcast(I32))
        nc.sync.dma_start(out=raw[1][:], in_=query2.rearrange("(p j) w -> p j w", j=PACK))
        nc.sync.dma_start(out=words[1][:].bitcast(I32), in_=keys_words[0, :, T : 2 * T].bitcast(I32))
        nc.sync.dma_start(out=list1[:], in_=offs)
        nc.sync.dma_start(out=list2[:], in_=offs2)
        nc.sync.dma_start(out=lam_col[:], in_=lam)
        nc.sync.dma_start(out=old_sb[:], in_=old)
        nc.sync.dma_start(out=list3[:], in_=offs3)
        nc.vector.memset(f1[:], 0.0)


        ident = sb.tile([P, P], F32, name="ident")
        make_identity(nc, ident[:])
        scores = []
        stationary = []
        for j in range(2):
            grouped = sb.tile([P, Q, PACK], BF16, name=f"grouped{j}", align_bytes=64)
            codes = sb.tile([P, Q], U32, name=f"codes{j}", align_bytes=64)
            q_scales = sb.tile([P, Q], U8, name=f"q_scales{j}", align_bytes=64)
            pieces = [slice(0, Q // 2), slice(Q // 2, Q)]
            nc.vector.tensor_copy(out=grouped[:, pieces[0], :], in_=raw[j][:, :, pieces[0]].rearrange("p j w -> p w j"))
            nc.scalar.activation(
                out=grouped[:, pieces[1], :], in_=raw[j][:, :, pieces[1]].rearrange("p j w -> p w j"), func=COPY
            )
            for rows in reversed(pieces):
                nc.vector.quantize_mx(
                    out=codes[:, rows].bitcast(FP8X4),
                    scales=q_scales[:, rows],
                    in_=grouped[:, rows, :].rearrange("p w j -> p (w j)"),
                )
            stationary.append((codes, q_scales))

        for j, (codes, q_scales) in enumerate(stationary):
            score = sb.tile([P, T], F32, name=f"score{j}")
            for n0 in range(0, T, N_TILE):
                acc = psum.tile([P, N_TILE], F32, name=f"acc{j}_{n0}")
                nc.tensor.matmul_mx(
                    out=acc[:],
                    lhsT=codes[:].bitcast(FP8X4),
                    lhsT_scale=q_scales[:],
                    rhs=words[2 * n0 // T][:, 2 * n0 % T : 2 * n0 % T + 2 * N_TILE].bitcast(FP4X4),
                    rhs_scale=key_scales[:, n0 : n0 + N_TILE],
                    start=True,
                    stop=True,
                )
                if j == 0 and n0 == T - 2 * N_TILE:
                    nc.vector.tensor_copy(out=score[:, n0 : n0 + N_TILE], in_=acc[:])
                else:
                    nc.scalar.activation(out=score[:, n0 : n0 + N_TILE], in_=acc[:], func=COPY)
            scores.append(score)
        a, b = scores

        cols = [slice(h * LIST_COLS, (h + 1) * LIST_COLS) for h in range(2)]
        slots = [slice(h * HALF, (h + 1) * HALF) for h in range(2)]
        from_a = [
            sb.tile([P, 2, HALF], F32, name="from_a0", tag="a_then_lam"),
            sb.tile([P, 2, HALF], F32, name="from_a1", tag="words_then_a", align_bytes=64),
        ]
        from_b = [
            sb.tile([P, 2, HALF], F32, name="from_b0"),
            sb.tile([P, 2, HALF], F32, name="from_b1", tag="b_then_old"),
        ]
        larger = [sb.tile([P, 2, HALF], F32, name=f"larger{h}") for h in range(2)]
        diff = sb.tile([P, HALF], F32, name="diff")
        lists = [list1, list2]
        for s in range(2):
            nc.vector.tensor_copy(out=from_a[0][:, s, :], in_=a[:].indirect(lists[s][:, cols[0]]))
        for s in range(2):
            nc.vector.tensor_copy(out=from_b[0][:, s, :], in_=b[:].indirect(lists[1 - s][:, cols[0]]))
        for s in range(2):
            nc.scalar.activation(out=from_a[1][:, s, :], in_=a[:].indirect(lists[s][:, cols[1]]), func=COPY)
            nc.scalar.activation(out=from_b[1][:, s, :], in_=b[:].indirect(lists[1 - s][:, cols[1]]), func=COPY)

        def take_larger(h, s):
            nc.vector.tensor_tensor(out=larger[h][:, s, :], in0=from_a[h][:, s, :], in1=from_b[h][:, s, :], op=ALU.max)

        w = sb.tile([P, I], F32, name="w")
        take_larger(0, 0)
        take_larger(0, 1)
        lam_wide = sb.tile([P, HALF], F32, name="lam_wide", tag="a_then_lam")
        nc.scalar.activation(out=lam_wide[:], in_=lam_col[:].to_broadcast([P, HALF]), func=COPY)
        take_larger(1, 0)
        nc.vector.tensor_tensor(out=diff[:], in0=larger[0][:, 0, :], in1=larger[0][:, 1, :], op=ALU.subtract)
        take_larger(1, 1)
        nc.vector.tensor_tensor(out=f1[:].indirect(list1[:, cols[0]]), in0=diff[:], in1=lam_wide[:], op=ALU.mult)
        minus_lam = sb.tile([P, 1], F32, name="minus_lam")
        nc.scalar.activation(out=minus_lam[:], in_=lam_wide[:, 0:1], func=COPY, scale=-1.0)
        terms = sb.tile([P, 2, HALF], F32, name="terms")
        nc.scalar.activation(out=terms[:, 0, :], in_=larger[1][:, 0, :], func=COPY, scale=lam_col[:])
        nc.scalar.activation(out=terms[:, 1, :], in_=larger[1][:, 1, :], func=COPY, scale=minus_lam[:])
        nc.scalar.activation(out=w[:, slots[0]], in_=diff[:], func=COPY, scale=lam_col[:])
        spans = [(0, 512), (512, 640)]
        old_turned = sb.tile([P, 640], F32, name="old_turned", tag="b_then_old")
        old_psum = []
        for u, (c0, c1) in enumerate(spans):
            turned = psum.tile([P, c1 - c0], F32, name=f"turned{u}", tag=f"acc0_{256 * u}")
            for c in range(c0, c1, P):
                nc.tensor.transpose(turned[:, c - c0 : c - c0 + P], old_sb[:, c : c + P], ident[:])
            nc.scalar.activation(out=old_turned[:, c0:c1], in_=turned[:], func=COPY)
        for u, (c0, c1) in enumerate(spans):
            back = psum.tile([P, c1 - c0], F32, name=f"back{u}", tag=f"acc0_{256 * (u + 2)}")
            for c in range(c0, c1, P):
                nc.tensor.transpose(back[:, c - c0 : c - c0 + P], old_turned[:, c : c + P], ident[:])
            old_psum.append(back)
        nc.vector.tensor_tensor(out=w[:, slots[1]], in0=terms[:, 0, :], in1=terms[:, 1, :], op=ALU.add)
        nc.vector.tensor_tensor(
            out=f1[:].indirect(list1[:, cols[1]]), in0=terms[:, 0, :], in1=terms[:, 1, :], op=ALU.add
        )

        f2 = sb.tile([P, T], F32, name="f2")
        nc.gpsimd.tensor_tensor(out=f2[:, 640:T], in0=f1[:, 640:T], in1=old_sb[:, 640:T], op=ALU.add)
        for (c0, c1), back in zip(spans, old_psum):
            nc.vector.tensor_tensor(out=f2[:, c0:c1], in0=f1[:, c0:c1], in1=back[:], op=ALU.add)

        res0 = sb.tile([P, HALF], F32, name="res0")
        res1 = sb.tile([P, HALF], F32, name="res1")
        picked = sb.tile([P, HALF], F32, name="picked")
        nc.vector.tensor_tensor(out=res0[:], in0=f2[:].indirect(list3[:, 0:LIST_COLS]), in1=w[:, 0:HALF], op=ALU.mult)
        nc.scalar.activation(out=picked[:], in_=f2[:].indirect(list3[:, LIST_COLS : 2 * LIST_COLS]), func=COPY)
        nc.sync.dma_start(out=out[:, 0:HALF], in_=res0[:])
        nc.vector.tensor_tensor(out=res1[:], in0=picked[:], in1=w[:, HALF:I], op=ALU.mult)
        nc.sync.dma_start(out=out[:, HALF:I], in_=res1[:])
